import numpy as np
import ml_dtypes


def mxq(x, axis, fmt="e4m3"):
    dtype, down = {"e4m3": (ml_dtypes.float8_e4m3fn, 7), "e5m2": (ml_dtypes.float8_e5m2, 14)}[fmt]
    v = np.moveaxis(np.asarray(x, np.float32).astype(ml_dtypes.bfloat16).astype(np.float64), axis, -1)
    blocks = v.reshape(v.shape[:-1] + (-1, 32))
    amax = np.abs(blocks).max(-1, keepdims=True)
    byte = np.maximum(np.where(amax > 0, np.frexp(amax)[1] - 1 + 127, 0) - down, 1)
    scale = np.exp2(byte - 127.0)
    codes = (blocks / scale).astype(np.float32).astype(dtype).astype(np.float64)
    return np.moveaxis((codes * scale).reshape(v.shape), -1, axis)


WIDE = False


def mx_kscale(k):
    if not WIDE:
        return np.ones(k)
    levels = np.array([10, -10, 5, -5, 0])
    if k % 512:
        return np.exp2(np.random.permutation(np.resize(levels, k // 32))).repeat(32)
    a = np.empty((k // 512, 16))
    for p in range(k // 512):
        a[p, :8] = np.random.permutation(np.resize(levels, 8))
        for g in range(8):
            far = levels[np.abs(levels - a[p, g]) >= 10]
            a[p, g + 8] = far[np.random.randint(len(far))]
    return np.exp2(a.ravel()).repeat(32)


def f64(x):
    return np.asarray(x).astype(np.float64)


def striped(idx):
    return np.tile(idx.reshape(-1, 16).T, (8, 1)).astype(np.uint16)


def unstriped(offs):
    return offs[:16].T.reshape(-1).astype(np.int64)


E2M1 = np.array([0.0, 0.5, 1.0, 1.5, 2.0, 3.0, 4.0, 6.0, -0.0, -0.5, -1.0, -1.5, -2.0, -3.0, -4.0, -6.0])


def pack_weight(w, fmt):
    k, n = w.shape
    w = f64(np.asarray(w, np.float32).astype(ml_dtypes.bfloat16)).reshape(k // 32, 32, n)
    amax = np.abs(w).max(1)
    if fmt == "e4m3":
        byte = np.frexp(amax)[1] - 1 + 127 - 7
    else:
        mant, ex = np.frexp(amax / 6.0)
        byte = np.where(mant > 0.5, ex, ex - 1) + 127
    byte = np.clip(np.where(amax > 0, byte, 1), 1, 254)
    scaled = (w * np.exp2(127.0 - byte)[:, None, :]).reshape(k, n).astype(np.float32)
    by_word = np.ascontiguousarray(scaled.reshape(k // 512, 128, 4, n).transpose(0, 1, 3, 2))
    if fmt == "e4m3":
        words = by_word.astype(ml_dtypes.float8_e4m3fn).view(np.uint8)
    else:
        c = by_word.astype(ml_dtypes.float4_e2m1fn).view(np.uint8) & 0xF
        words = (c[..., 0::2] | (c[..., 1::2] << 4)).reshape(k // 512, 128, 2 * n)
    return np.ascontiguousarray(words), np.ascontiguousarray(byte.astype(np.uint8).reshape(k // 512, 16, n))


def unpack_weight(words, scales, fmt):
    g, _, n = scales.shape
    words = np.ascontiguousarray(words).reshape(g, 128, n, -1)
    if fmt == "e4m3":
        vals = words.view(ml_dtypes.float8_e4m3fn).astype(np.float64)
    else:
        nib = np.empty((g, 128, n, 4), np.uint8)
        nib[..., 0::2] = words & 0xF
        nib[..., 1::2] = words >> 4
        vals = E2M1[nib]
    vals = vals * np.repeat(np.exp2(scales.astype(np.float64) - 127.0), 8, axis=1)[..., None]
    return vals.transpose(0, 1, 3, 2).reshape(g * 512, n)


def d_relu2(v):
    return 2.0 * np.maximum(v, 0.0)


K, T, G, C1, E, C2, H = 256, 1024, 2, 512, 8, 128, 512
N = 1024


def by_expert(wq, xq, E, C):
    return np.concatenate([wq[e].T @ xq[:, e * C:(e + 1) * C] for e in range(E)], axis=1)


def setup_inputs():
    n = np.random.standard_normal
    v = mx_kscale(N)
    u = mx_kscale(H)
    slots1 = np.random.permutation(T)
    slots2 = np.concatenate([q * C1 + np.random.permutation(C1) for q in range(G)])
    dy = pack_weight(n((N, T)) * v[:, None], "e4m3")
    wet = [pack_weight(m, "e2m1") for m in n((E, N, H)) / np.sqrt(N) / v[None, :, None] * u]
    wgt = [pack_weight(m, "e4m3") for m in n((G, H, K)) / np.sqrt(H) / u[None, :, None]]
    return {
        "dy_words": dy[0],
        "dy_scales": dy[1],
        "wet_words": np.stack([m[0] for m in wet]),
        "wet_scales": np.stack([m[1] for m in wet]),
        "wgt_words": np.stack([m[0] for m in wgt]),
        "wgt_scales": np.stack([m[1] for m in wgt]),
        "a": (n((H, T))).astype(np.float32),
        "gate": (np.tile(np.random.uniform(0.2, 1.0, T), (128, 1))).astype(np.float32),
        "offs": striped(slots1),
        "offs2": striped(slots2),
        "dst": striped(slots1[slots2]),
    }


def reference(dy_words, dy_scales, wet_words, wet_scales, wgt_words, wgt_scales, a, gate, offs, offs2, dst):
    wet = np.stack([unpack_weight(wet_words[e], wet_scales[e], "e2m1") for e in range(E)])
    wgt = np.stack([unpack_weight(wgt_words[e], wgt_scales[e], "e4m3") for e in range(G)])
    gq = unpack_weight(dy_words, dy_scales, "e4m3")[:, unstriped(dst)]
    z = f64(gate[:1]) * by_expert(wet, gq, E, C2)
    da = np.zeros((H, T))
    da[:, unstriped(offs2)] = z
    dx = by_expert(wgt, mxq(da * d_relu2(f64(a)), 0, "e4m3"), G, C1)
    out = np.zeros((K, T))
    out[:, unstriped(offs)] = dx
    return out

@@ -1,0 +1,251 @@
+from contextlib import ExitStack
+
+import concourse.mybir as mybir
+from concourse.masks import make_identity
+
+K, T, G, C1, E, C2, H, N = 256, 1024, 2, 512, 8, 128, 512, 1024
+FLOPS = 2 * T * H * (N + K)
+
+F32 = mybir.dt.float32
+BF16 = mybir.dt.bfloat16
+I32 = mybir.dt.int32
+U32 = mybir.dt.uint32
+U16 = mybir.dt.uint16
+U8 = mybir.dt.uint8
+FP8X4 = mybir.dt.float8_e4m3fn_x4
+FP4X4 = mybir.dt.float4_e2m1fn_x4
+COPY = mybir.ActivationFunctionType.Copy
+RELU = mybir.ActivationFunctionType.Relu
+MULT = mybir.AluOpType.mult
+
+P = 128
+PACK = 4
+PASSES = N // 512
+EG = E // G
+HALF = C1 // 2
+
+
+def cols(first, count):
+    return slice(first // 16, (first + count) // 16)
+
+
+def tile_moe_hib_relu2_kernel(
+    tc, dy_words, dy_scales, wet_words, wet_scales, wgt_words, wgt_scales, a, gate, offs, offs2, dst, out
+):
+    nc = tc.nc
+    with ExitStack() as ctx:
+        lists = ctx.enter_context(tc.tile_pool(name="lists", bufs=1))
+        sb = ctx.enter_context(tc.tile_pool(name="sb", bufs=1))
+        psum = ctx.enter_context(tc.psum_pool(name="psum", bufs=1))
+
+        def tile(name, shape, dtype, tag=None):
+            return sb.tile(shape, dtype, name=name, tag=tag or name, align_bytes=64)
+
+        def bank(name, shape, number):
+            return psum.tile(shape, F32, name=name, tag="bank%d" % number)
+
+        dst_t = lists.tile([P, T // 16], U16, name="dst_t")
+        offs2_t = lists.tile([P, T // 16], U16, name="offs2_t")
+        offs_t = lists.tile([P, T // 16], U16, name="offs_t")
+
+        dy_s = tile("dy_s", [P, T], U8)
+        we_s = {}
+        gate_rows = tile("gate_rows", [P, P], F32)
+        ident = tile("ident", [P, P], F32)
+        nc.gpsimd.memset(dy_s[:].bitcast(I32), 0)
+        nc.gpsimd.memset(gate_rows[:], 0.0)
+        nc.gpsimd.dma_start(out=gate_rows[0:E, :], in_=gate[0, :].rearrange("(e m) -> e m", e=E))
+        make_identity(nc, ident[:])
+
+        def load_expert_words(name, first, count, tag=None):
+            t = tile(name, [P, count * PASSES, 2 * H], U8, tag)
+            nc.sync.dma_start(
+                out=t[:].bitcast(I32),
+                in_=wet_words[first : first + count].rearrange("e s p b -> p (e s) b").bitcast(I32),
+            )
+            return t
+
+        def load_expert_scales(g, tag=None):
+            we_s[g] = tile("we_s%d" % g, [P, EG * PASSES, H], U8, tag)
+            for r in range(4):
+                nc.sync.dma_start(
+                    out=we_s[g][r:P:32, :, :].bitcast(I32),
+                    in_=wet_scales[EG * g : EG * (g + 1), :, r:16:4, :].rearrange("e s q i -> q (e s) i").bitcast(I32),
+                )
+
+        def load_a(g, tag):
+            t = tile("a%d" % g, [P, PACK, C1], F32, tag)
+            nc.sync.dma_start(out=t[:], in_=a[:, C1 * g : C1 * (g + 1)].rearrange("(p t) j -> p t j", t=PACK))
+            return t
+
+        nc.sync.dma_start(dst_t[:], dst)
+        for q in range(4):
+            nc.sync.dma_start(
+                out=dy_s[32 * q : 32 * q + 8, :].bitcast(I32),
+                in_=dy_scales[:, 4 * q : 4 * q + 4, :].bitcast(I32),
+            )
+        dy_w = []
+        for s in range(PASSES):
+            t = tile("dy_w%d" % s, [P, T], U32)
+            nc.sync.dma_start(out=t[:].bitcast(I32), in_=dy_words[s].rearrange("p t d -> p (t d)").bitcast(I32))
+            dy_w.append(t)
+        we_w = {}
+        we_w[0] = load_expert_words("we_w01", 0, 2)
+        load_expert_scales(0)
+        we_w[2] = load_expert_words("we_w23", 2, 2)
+        nc.sync.dma_start(offs2_t[:], offs2)
+        nc.sync.dma_start(offs_t[:], offs)
+
+        gate_ps = bank("gate_ps", [P, P], 7)
+        nc.tensor.transpose(gate_ps[:], gate_rows[:], ident[:])
+        gate2 = tile("gate2", [P, E], F32)
+        nc.scalar.activation(gate2[:], gate_ps[:, 0:E], COPY, scale=2.0)
+
+        g_w = [tile("g_w%d" % s, [P, T], U32) for s in range(PASSES)]
+        g_s = [tile("g_s%d" % s, [P, T], U8) for s in range(PASSES)]
+
+        def gather_words(s, first, count):
+            nc.vector.tensor_copy(g_w[s][:, first : first + count], dy_w[s][:].indirect(dst_t[:, cols(first, count)]))
+
+        def gather_scales(first, count):
+            nc.vector.tensor_copy(g_s[0][:, first : first + count], dy_s[:].indirect(dst_t[:, cols(first, count)]))
+
+        for g, queue in ((0, nc.scalar), (1, nc.gpsimd)):
+            slots = slice(C1 * g, C1 * (g + 1))
+            gather_scales(C1 * g, C1)
+            for r in range(4):
+                queue.dma_start(out=g_s[1][r:P:32, slots].bitcast(I32), in_=g_s[0][4 + r : P : 32, slots].bitcast(I32))
+            for s in range(PASSES):
+                gather_words(s, C1 * g, C1)
+
+        z_slots = [tile("z_slots%d" % g, [P, PACK, C1], F32) for g in range(G)]
+        z_rows = {}
+
+        def expert_product(e, words, first):
+            acc = bank("acc%d" % e, [P, H], e % EG)
+            slots = slice(C2 * e, C2 * (e + 1))
+            for s in range(PASSES):
+                nc.tensor.matmul_mx(
+                    out=acc[:],
+                    lhsT=g_w[s][:, slots].bitcast(FP8X4),
+                    lhsT_scale=g_s[s][:, slots],
+                    rhs=words[:, (e - first) * PASSES + s, :].bitcast(FP4X4),
+                    rhs_scale=we_s[e // EG][:, (e % EG) * PASSES + s, :],
+                    start=(s == 0),
+                    stop=(s == PASSES - 1),
+                )
+            z_rows[e] = tile("z_rows%d" % e, [P, PACK, P], F32)
+            nc.scalar.activation(
+                z_rows[e][:], acc[:].rearrange("m (q t) -> m t q", t=PACK), COPY, scale=gate2[:, e : e + 1]
+            )
+
+        def turn(e):
+            turned = bank("turned%d" % e, [P, PACK, C2], EG + e % EG)
+            for t in range(PACK):
+                nc.tensor.transpose(turned[:, t, :], z_rows[e][:, t, :], ident[:])
+            u = C2 * (e % EG)
+            nc.scalar.copy(z_slots[e // EG][:, :, u : u + C2], turned[:])
+
+        def experts(g, words_of):
+            for e in range(EG * g, EG * (g + 1)):
+                expert_product(e, *words_of(e))
+                if e % EG:
+                    turn(e - 1)
+            turn(EG * (g + 1) - 1)
+
+        experts(0, lambda e: (we_w[e - e % 2], e - e % 2))
+        load_expert_scales(1, tag="z_rows1")
+        we_w[EG] = load_expert_words("we_w47", EG, EG, tag="z_rows3")
+        experts(1, lambda e: (we_w[EG], EG))
+        a_t = [load_a(0, "z_rows4"), load_a(1, "z_rows6")]
+        slope = [tile("slope%d" % g, [P, PACK, C1], F32) for g in range(G)]
+        for g in range(G):
+            for t in range(PACK):
+                nc.scalar.activation(slope[g][:, t, :], a_t[g][:, t, :], RELU)
+        wg_w = tile("wg_w", [P, G, K], U32, "z_rows5")
+        nc.sync.dma_start(out=wg_w[:].bitcast(I32), in_=wgt_words[:, 0].rearrange("f p k d -> p f (k d)").bitcast(I32))
+
+        wg_s = tile("wg_s", [P, G, K], U8, "z_rows0")
+        for r in range(4):
+            nc.sync.dma_start(
+                out=wg_s[r:P:32, :, :].bitcast(I32),
+                in_=wgt_scales[:, 0, r:16:4, :].rearrange("f q k -> q f k").bitcast(I32),
+            )
+
+        window = {}
+        da = [tile("da%d" % g, [P, PACK, C1], BF16) for g in range(G)]
+        woven = {}
+        codes = {}
+        planes = {}
+        dx = {}
+        rows_out = {}
+
+        def scatter_z(g, t, first, count, tag=None):
+            if (g, t) not in window:
+                window[g, t] = tile("window%d%d" % (g, t), [P, T], F32, tag)
+            nc.vector.tensor_copy(
+                window[g, t][:].indirect(offs2_t[:, cols(C1 * g + first, count)]), z_slots[g][:, t, first : first + count]
+            )
+
+        def times_slope(g, t, first=0, count=C1):
+            j = slice(first, first + count)
+            nc.gpsimd.tensor_tensor(
+                da[g][:, t, j], slope[g][:, t, j], window[g, t][:, C1 * g + first : C1 * g + first + count], MULT
+            )
+
+        def weave(g, tag):
+            woven[g] = tile("woven%d" % g, [P, C1, PACK], BF16, tag)
+            for h in range(2):
+                j = slice(HALF * h, HALF * (h + 1))
+                nc.scalar.copy(woven[g][:, j, :], da[g][:, :, j].rearrange("p t j -> p j t"))
+
+        def group_product(g):
+            codes[g] = tile("codes%d" % g, [P, C1], U32)
+            planes[g] = tile("planes%d" % g, [P, C1], U8)
+            nc.vector.quantize_mx(
+                out=codes[g][:].bitcast(FP8X4), scales=planes[g][:], in_=woven[g][:].rearrange("p j t -> p (j t)")
+            )
+            for b in range(K // P):
+                acc = bank("dx_ps%d%d" % (g, b), [P, C1], 2 * g + b)
+                nc.tensor.matmul_mx(
+                    out=acc[:],
+                    lhsT=wg_w[:, g, P * b : P * (b + 1)].bitcast(FP8X4),
+                    lhsT_scale=wg_s[:, g, P * b : P * (b + 1)],
+                    rhs=codes[g][:].bitcast(FP8X4),
+                    rhs_scale=planes[g][:],
+                    start=True,
+                    stop=True,
+                )
+                dx[g, b] = tile("dx%d%d" % (g, b), [P, C1], F32)
+                nc.scalar.copy(dx[g, b][:], acc[:])
+
+        def scatter_dx(g, b, tag=None):
+            if b not in rows_out:
+                rows_out[b] = tile("rows_out%d" % b, [P, T], F32, tag)
+            nc.vector.tensor_copy(rows_out[b][:].indirect(offs_t[:, cols(C1 * g, C1)]), dx[g, b][:])
+
+        for t in range(PACK):
+            scatter_z(0, t, 0, C2)
+        for t in range(PACK):
+            scatter_z(0, t, C2, C1 - C2)
+            if t:
+                times_slope(0, t - 1)
+        scatter_z(1, 0, 0, C1)
+        times_slope(0, PACK - 1)
+        weave(0, "z_rows7")
+        scatter_z(1, 1, 0, C1)
+        times_slope(1, 0)
+        scatter_z(1, 2, 0, C1)
+        times_slope(1, 1)
+        group_product(0)
+        scatter_z(1, 3, 0, C1, tag="z_rows7")
+        times_slope(1, 2)
+        times_slope(1, 3, 0, HALF)
+        times_slope(1, 3, HALF, HALF)
+        weave(1, "codes0")
+        scatter_dx(0, 0)
+        group_product(1)
+        scatter_dx(0, 1, tag="codes0")
+        for b in range(K // P):
+            scatter_dx(1, b)
+            nc.sync.dma_start(out=out[P * b : P * (b + 1), :], in_=rows_out[b][:])

@@ -53,9 +53,9 @@ def tile_moe_hib_relu2_kernel(
         gate_rows = tile("gate_rows", [P, P], F32)
         ident = tile("ident", [P, P], F32)
         nc.gpsimd.memset(dy_s[:].bitcast(I32), 0)
-        nc.gpsimd.memset(gate_rows[:], 0.0)
-        nc.gpsimd.dma_start(out=gate_rows[0:E, :], in_=gate[0, :].rearrange("(e m) -> e m", e=E))
         make_identity(nc, ident[:])
+        nc.scalar.activation(gate_rows[:], ident[:], COPY, scale=0.0)
+        nc.scalar.dma_start(out=gate_rows[0:E, :], in_=gate[0, :].rearrange("(e m) -> e m", e=E))
 
         def load_expert_words(name, first, count, tag=None):
             t = tile(name, [P, count * PASSES, 2 * H], U8, tag)
@@ -84,16 +84,12 @@ def tile_moe_hib_relu2_kernel(
                 out=dy_s[32 * q : 32 * q + 8, :].bitcast(I32),
                 in_=dy_scales[:, 4 * q : 4 * q + 4, :].bitcast(I32),
             )
-        dy_w = []
-        for s in range(PASSES):
-            t = tile("dy_w%d" % s, [P, T], U32)
-            nc.sync.dma_start(out=t[:].bitcast(I32), in_=dy_words[s].rearrange("p t d -> p (t d)").bitcast(I32))
-            dy_w.append(t)
+        nc.sync.dma_start(offs2_t[:], offs2)
+        dy_w = tile("dy_w", [P, PASSES, T], U32)
+        nc.sync.dma_start(out=dy_w[:].bitcast(I32), in_=dy_words.rearrange("s p t d -> p s (t d)").bitcast(I32))
         we_w = {}
         we_w[0] = load_expert_words("we_w01", 0, 2)
         load_expert_scales(0)
-        we_w[2] = load_expert_words("we_w23", 2, 2)
-        nc.sync.dma_start(offs2_t[:], offs2)
         nc.sync.dma_start(offs_t[:], offs)
 
         gate_ps = bank("gate_ps", [P, P], 7)
@@ -105,24 +101,25 @@ def tile_moe_hib_relu2_kernel(
         g_s = [tile("g_s%d" % s, [P, T], U8) for s in range(PASSES)]
 
         def gather_words(s, first, count):
-            nc.vector.tensor_copy(g_w[s][:, first : first + count], dy_w[s][:].indirect(dst_t[:, cols(first, count)]))
+            nc.vector.tensor_copy(g_w[s][:, first : first + count], dy_w[:, s, :].indirect(dst_t[:, cols(first, count)]))
 
         def gather_scales(first, count):
             nc.vector.tensor_copy(g_s[0][:, first : first + count], dy_s[:].indirect(dst_t[:, cols(first, count)]))
 
-        for g, queue in ((0, nc.scalar), (1, nc.gpsimd)):
+        for g, queue in enumerate((nc.scalar, nc.sync)):
             slots = slice(C1 * g, C1 * (g + 1))
             gather_scales(C1 * g, C1)
-            for r in range(4):
-                queue.dma_start(out=g_s[1][r:P:32, slots].bitcast(I32), in_=g_s[0][4 + r : P : 32, slots].bitcast(I32))
+            queue.dma_start(out=g_s[1][0:112, slots].bitcast(I32), in_=g_s[0][4:116, slots].bitcast(I32))
+        we_w[2] = load_expert_words("we_w23", 2, 2, tag="dy_s")
+        for first, count in ((0, C2), (C2, C1 - C2), (C1, C1)):
             for s in range(PASSES):
-                gather_words(s, C1 * g, C1)
+                gather_words(s, first, count)
 
         z_slots = [tile("z_slots%d" % g, [P, PACK, C1], F32) for g in range(G)]
         z_rows = {}
 
         def expert_product(e, words, first):
-            acc = bank("acc%d" % e, [P, H], e % EG)
+            acc = bank("acc%d" % e, [P, H], (0, 0, 4, 0, 1, 2, 3, 0)[e])
             slots = slice(C2 * e, C2 * (e + 1))
             for s in range(PASSES):
                 nc.tensor.matmul_mx(
@@ -149,15 +146,17 @@ def tile_moe_hib_relu2_kernel(
         def experts(g, words_of):
             for e in range(EG * g, EG * (g + 1)):
                 expert_product(e, *words_of(e))
-                if e % EG:
+                if e == 0:
+                    turn(e)
+                elif e % EG and e != 1:
                     turn(e - 1)
             turn(EG * (g + 1) - 1)
 
         experts(0, lambda e: (we_w[e - e % 2], e - e % 2))
-        load_expert_scales(1, tag="z_rows1")
-        we_w[EG] = load_expert_words("we_w47", EG, EG, tag="z_rows3")
+        load_expert_scales(1, tag="we_w01")
+        we_w[EG] = load_expert_words("we_w47", EG, EG, tag="z_rows0")
         experts(1, lambda e: (we_w[EG], EG))
-        a_t = [load_a(0, "z_rows4"), load_a(1, "z_rows6")]
+        a_t = [load_a(0, "z_rows2"), load_a(1, "z_rows4")]
         slope = [tile("slope%d" % g, [P, PACK, C1], F32) for g in range(G)]
         for g in range(G):
             for t in range(PACK):
@@ -165,7 +164,7 @@ def tile_moe_hib_relu2_kernel(
         wg_w = tile("wg_w", [P, G, K], U32, "z_rows5")
         nc.sync.dma_start(out=wg_w[:].bitcast(I32), in_=wgt_words[:, 0].rearrange("f p k d -> p f (k d)").bitcast(I32))
 
-        wg_s = tile("wg_s", [P, G, K], U8, "z_rows0")
+        wg_s = tile("wg_s", [P, G, K], U8, "z_rows3")
         for r in range(4):
             nc.sync.dma_start(
                 out=wg_s[r:P:32, :, :].bitcast(I32),
@@ -206,7 +205,7 @@ def tile_moe_hib_relu2_kernel(
                 out=codes[g][:].bitcast(FP8X4), scales=planes[g][:], in_=woven[g][:].rearrange("p j t -> p (j t)")
             )
             for b in range(K // P):
-                acc = bank("dx_ps%d%d" % (g, b), [P, C1], 2 * g + b)
+                acc = bank("dx_ps%d%d" % (g, b), [P, C1], 2 + b)
                 nc.tensor.matmul_mx(
                     out=acc[:],
                     lhsT=wg_w[:, g, P * b : P * (b + 1)].bitcast(FP8X4),
@@ -224,10 +223,11 @@ def tile_moe_hib_relu2_kernel(
                 rows_out[b] = tile("rows_out%d" % b, [P, T], F32, tag)
             nc.vector.tensor_copy(rows_out[b][:].indirect(offs_t[:, cols(C1 * g, C1)]), dx[g, b][:])
 
+        for first in (0, C2):
+            for t in range(PACK):
+                scatter_z(0, t, first, C2)
         for t in range(PACK):
-            scatter_z(0, t, 0, C2)
-        for t in range(PACK):
-            scatter_z(0, t, C2, C1 - C2)
+            scatter_z(0, t, HALF, HALF)
             if t:
                 times_slope(0, t - 1)
         scatter_z(1, 0, 0, C1)

@@ -53,9 +53,9 @@ def tile_moe_hib_relu2_kernel(
         gate_rows = tile("gate_rows", [P, P], F32)
         ident = tile("ident", [P, P], F32)
         nc.gpsimd.memset(dy_s[:].bitcast(I32), 0)
-        make_identity(nc, ident[:])
-        nc.scalar.activation(gate_rows[:], ident[:], COPY, scale=0.0)
+        nc.gpsimd.memset(gate_rows[:], 0.0)
         nc.scalar.dma_start(out=gate_rows[0:E, :], in_=gate[0, :].rearrange("(e m) -> e m", e=E))
+        make_identity(nc, ident[:])
 
         def load_expert_words(name, first, count, tag=None):
             t = tile(name, [P, count * PASSES, 2 * H], U8, tag)
@@ -88,7 +88,7 @@ def tile_moe_hib_relu2_kernel(
         dy_w = tile("dy_w", [P, PASSES, T], U32)
         nc.sync.dma_start(out=dy_w[:].bitcast(I32), in_=dy_words.rearrange("s p t d -> p s (t d)").bitcast(I32))
         we_w = {}
-        we_w[0] = load_expert_words("we_w01", 0, 2)
+        we_w[0] = load_expert_words("we_w0", 0, 1)
         load_expert_scales(0)
         nc.sync.dma_start(offs_t[:], offs)
 
@@ -98,7 +98,7 @@ def tile_moe_hib_relu2_kernel(
         nc.scalar.activation(gate2[:], gate_ps[:, 0:E], COPY, scale=2.0)
 
         g_w = [tile("g_w%d" % s, [P, T], U32) for s in range(PASSES)]
-        g_s = [tile("g_s%d" % s, [P, T], U8) for s in range(PASSES)]
+        g_s = [tile("g_s0", [P, T], U8), tile("g_s1", [P, T], U8, "gate_rows")]
 
         def gather_words(s, first, count):
             nc.vector.tensor_copy(g_w[s][:, first : first + count], dy_w[:, s, :].indirect(dst_t[:, cols(first, count)]))
@@ -110,7 +110,7 @@ def tile_moe_hib_relu2_kernel(
             slots = slice(C1 * g, C1 * (g + 1))
             gather_scales(C1 * g, C1)
             queue.dma_start(out=g_s[1][0:112, slots].bitcast(I32), in_=g_s[0][4:116, slots].bitcast(I32))
-        we_w[2] = load_expert_words("we_w23", 2, 2, tag="dy_s")
+        we_w[1] = load_expert_words("we_w13", 1, 3, tag="dy_s")
         for first, count in ((0, C2), (C2, C1 - C2), (C1, C1)):
             for s in range(PASSES):
                 gather_words(s, first, count)
@@ -132,9 +132,12 @@ def tile_moe_hib_relu2_kernel(
                     stop=(s == PASSES - 1),
                 )
             z_rows[e] = tile("z_rows%d" % e, [P, PACK, P], F32)
-            nc.scalar.activation(
-                z_rows[e][:], acc[:].rearrange("m (q t) -> m t q", t=PACK), COPY, scale=gate2[:, e : e + 1]
-            )
+            by_t = acc[:].rearrange("m (q t) -> m t q", t=PACK)
+            step = 2 if e == 0 else PACK
+            for t in range(0, PACK, step):
+                nc.scalar.activation(
+                    z_rows[e][:, t : t + step, :], by_t[:, t : t + step, :], COPY, scale=gate2[:, e : e + 1]
+                )
 
         def turn(e):
             turned = bank("turned%d" % e, [P, PACK, C2], EG + e % EG)
@@ -152,8 +155,8 @@ def tile_moe_hib_relu2_kernel(
                     turn(e - 1)
             turn(EG * (g + 1) - 1)
 
-        experts(0, lambda e: (we_w[e - e % 2], e - e % 2))
-        load_expert_scales(1, tag="we_w01")
+        experts(0, lambda e: (we_w[min(e, 1)], min(e, 1)))
+        load_expert_scales(1, tag="we_w0")
         we_w[EG] = load_expert_words("we_w47", EG, EG, tag="z_rows0")
         experts(1, lambda e: (we_w[EG], EG))
         a_t = [load_a(0, "z_rows2"), load_a(1, "z_rows4")]

@@ -175,8 +175,7 @@ def tile_moe_hib_relu2_kernel(
             )
 
         window = {}
-        da = [tile("da%d" % g, [P, PACK, C1], BF16) for g in range(G)]
-        woven = {}
+        woven = [tile("woven%d" % g, [P, C1, PACK], BF16) for g in range(G)]
         codes = {}
         planes = {}
         dx = {}
@@ -189,20 +188,13 @@ def tile_moe_hib_relu2_kernel(
                 window[g, t][:].indirect(offs2_t[:, cols(C1 * g + first, count)]), z_slots[g][:, t, first : first + count]
             )
 
-        def times_slope(g, t, first=0, count=C1):
-            j = slice(first, first + count)
+        def times_slope(g, t):
             nc.gpsimd.tensor_tensor(
-                da[g][:, t, j], slope[g][:, t, j], window[g, t][:, C1 * g + first : C1 * g + first + count], MULT
+                woven[g][:, :, t], slope[g][:, t, :], window[g, t][:, C1 * g : C1 * (g + 1)], MULT
             )
 
-        def weave(g, tag):
-            woven[g] = tile("woven%d" % g, [P, C1, PACK], BF16, tag)
-            for h in range(2):
-                j = slice(HALF * h, HALF * (h + 1))
-                nc.scalar.copy(woven[g][:, j, :], da[g][:, :, j].rearrange("p t j -> p j t"))
-
-        def group_product(g):
-            codes[g] = tile("codes%d" % g, [P, C1], U32)
+        def group_product(g, tag):
+            codes[g] = tile("codes%d" % g, [P, C1], U32, tag)
             planes[g] = tile("planes%d" % g, [P, C1], U8)
             nc.vector.quantize_mx(
                 out=codes[g][:].bitcast(FP8X4), scales=planes[g][:], in_=woven[g][:].rearrange("p j t -> p (j t)")
@@ -235,20 +227,17 @@ def tile_moe_hib_relu2_kernel(
                 times_slope(0, t - 1)
         scatter_z(1, 0, 0, C1)
         times_slope(0, PACK - 1)
-        weave(0, "z_rows7")
         scatter_z(1, 1, 0, C1)
         times_slope(1, 0)
         scatter_z(1, 2, 0, C1)
         times_slope(1, 1)
-        group_product(0)
-        scatter_z(1, 3, 0, C1, tag="z_rows7")
+        group_product(0, "window10")
+        scatter_z(1, 3, 0, C1, tag="woven0")
         times_slope(1, 2)
-        times_slope(1, 3, 0, HALF)
-        times_slope(1, 3, HALF, HALF)
-        weave(1, "codes0")
+        times_slope(1, 3)
         scatter_dx(0, 0)
-        group_product(1)
-        scatter_dx(0, 1, tag="codes0")
+        group_product(1, "dx00")
+        scatter_dx(0, 1, tag="woven1")
         for b in range(K // P):
             scatter_dx(1, b)
             nc.sync.dma_start(out=out[P * b : P * (b + 1), :], in_=rows_out[b][:])

from contextlib import ExitStack

import concourse.mybir as mybir
from concourse.masks import make_identity

K, T, G, C1, E, C2, H, N = 256, 1024, 2, 512, 8, 128, 512, 1024
FLOPS = 2 * T * H * (N + K)

F32 = mybir.dt.float32
BF16 = mybir.dt.bfloat16
I32 = mybir.dt.int32
U32 = mybir.dt.uint32
U16 = mybir.dt.uint16
U8 = mybir.dt.uint8
FP8X4 = mybir.dt.float8_e4m3fn_x4
FP4X4 = mybir.dt.float4_e2m1fn_x4
COPY = mybir.ActivationFunctionType.Copy
RELU = mybir.ActivationFunctionType.Relu
MULT = mybir.AluOpType.mult

P = 128
PACK = 4
PASSES = N // 512
EG = E // G
HALF = C1 // 2


def cols(first, count):
    return slice(first // 16, (first + count) // 16)


def tile_moe_hib_relu2_kernel(
    tc, dy_words, dy_scales, wet_words, wet_scales, wgt_words, wgt_scales, a, gate, offs, offs2, dst, out
):
    nc = tc.nc
    with ExitStack() as ctx:
        lists = ctx.enter_context(tc.tile_pool(name="lists", bufs=1))
        sb = ctx.enter_context(tc.tile_pool(name="sb", bufs=1))
        psum = ctx.enter_context(tc.psum_pool(name="psum", bufs=1))

        def tile(name, shape, dtype, tag=None):
            return sb.tile(shape, dtype, name=name, tag=tag or name, align_bytes=64)

        def bank(name, shape, number):
            return psum.tile(shape, F32, name=name, tag="bank%d" % number)

        dst_t = lists.tile([P, T // 16], U16, name="dst_t")
        offs2_t = lists.tile([P, T // 16], U16, name="offs2_t")
        offs_t = lists.tile([P, T // 16], U16, name="offs_t")

        dy_s = tile("dy_s", [P, T], U8)
        we_s = {}
        gate_rows = tile("gate_rows", [P, P], F32)
        ident = tile("ident", [P, P], F32)
        nc.gpsimd.memset(dy_s[:].bitcast(I32), 0)
        nc.gpsimd.memset(gate_rows[:], 0.0)
        nc.scalar.dma_start(out=gate_rows[0:E, :], in_=gate[0, :].rearrange("(e m) -> e m", e=E))
        make_identity(nc, ident[:])

        def load_expert_words(name, first, count, tag=None):
            t = tile(name, [P, count * PASSES, 2 * H], U8, tag)
            nc.sync.dma_start(
                out=t[:].bitcast(I32),
                in_=wet_words[first : first + count].rearrange("e s p b -> p (e s) b").bitcast(I32),
            )
            return t

        def load_expert_scales(g, tag=None):
            we_s[g] = tile("we_s%d" % g, [P, EG * PASSES, H], U8, tag)
            for r in range(4):
                nc.sync.dma_start(
                    out=we_s[g][r:P:32, :, :].bitcast(I32),
                    in_=wet_scales[EG * g : EG * (g + 1), :, r:16:4, :].rearrange("e s q i -> q (e s) i").bitcast(I32),
                )

        def load_a(g, tag):
            t = tile("a%d" % g, [P, PACK, C1], F32, tag)
            nc.sync.dma_start(out=t[:], in_=a[:, C1 * g : C1 * (g + 1)].rearrange("(p t) j -> p t j", t=PACK))
            return t

        nc.sync.dma_start(dst_t[:], dst)
        for q in range(4):
            nc.sync.dma_start(
                out=dy_s[32 * q : 32 * q + 8, :].bitcast(I32),
                in_=dy_scales[:, 4 * q : 4 * q + 4, :].bitcast(I32),
            )
        nc.sync.dma_start(offs2_t[:], offs2)
        dy_w = tile("dy_w", [P, PASSES, T], U32)
        nc.sync.dma_start(out=dy_w[:].bitcast(I32), in_=dy_words.rearrange("s p t d -> p s (t d)").bitcast(I32))
        we_w = {}
        we_w[0] = load_expert_words("we_w0", 0, 1)
        load_expert_scales(0)
        nc.sync.dma_start(offs_t[:], offs)

        gate_ps = bank("gate_ps", [P, P], 7)
        nc.tensor.transpose(gate_ps[:], gate_rows[:], ident[:])
        gate2 = tile("gate2", [P, E], F32)
        nc.scalar.activation(gate2[:], gate_ps[:, 0:E], COPY, scale=2.0)

        g_w = [tile("g_w%d" % s, [P, T], U32) for s in range(PASSES)]
        g_s = [tile("g_s0", [P, T], U8), tile("g_s1", [P, T], U8, "gate_rows")]

        def gather_words(s, first, count):
            nc.vector.tensor_copy(g_w[s][:, first : first + count], dy_w[:, s, :].indirect(dst_t[:, cols(first, count)]))

        def gather_scales(first, count):
            nc.vector.tensor_copy(g_s[0][:, first : first + count], dy_s[:].indirect(dst_t[:, cols(first, count)]))

        for g, queue in enumerate((nc.scalar, nc.sync)):
            slots = slice(C1 * g, C1 * (g + 1))
            gather_scales(C1 * g, C1)
            queue.dma_start(out=g_s[1][0:112, slots].bitcast(I32), in_=g_s[0][4:116, slots].bitcast(I32))
        we_w[1] = load_expert_words("we_w13", 1, 3, tag="dy_s")
        for first, count in ((0, C2), (C2, C1 - C2), (C1, C1)):
            for s in range(PASSES):
                gather_words(s, first, count)

        z_slots = [tile("z_slots%d" % g, [P, PACK, C1], F32) for g in range(G)]
        z_rows = {}

        def expert_product(e, words, first):
            acc = bank("acc%d" % e, [P, H], (0, 0, 4, 0, 1, 2, 3, 0)[e])
            slots = slice(C2 * e, C2 * (e + 1))
            for s in range(PASSES):
                nc.tensor.matmul_mx(
                    out=acc[:],
                    lhsT=g_w[s][:, slots].bitcast(FP8X4),
                    lhsT_scale=g_s[s][:, slots],
                    rhs=words[:, (e - first) * PASSES + s, :].bitcast(FP4X4),
                    rhs_scale=we_s[e // EG][:, (e % EG) * PASSES + s, :],
                    start=(s == 0),
                    stop=(s == PASSES - 1),
                )
            z_rows[e] = tile("z_rows%d" % e, [P, PACK, P], F32)
            by_t = acc[:].rearrange("m (q t) -> m t q", t=PACK)
            step = 2 if e == 0 else PACK
            for t in range(0, PACK, step):
                nc.scalar.activation(
                    z_rows[e][:, t : t + step, :], by_t[:, t : t + step, :], COPY, scale=gate2[:, e : e + 1]
                )

        def turn(e):
            turned = bank("turned%d" % e, [P, PACK, C2], EG + e % EG)
            for t in range(PACK):
                nc.tensor.transpose(turned[:, t, :], z_rows[e][:, t, :], ident[:])
            u = C2 * (e % EG)
            nc.scalar.copy(z_slots[e // EG][:, :, u : u + C2], turned[:])

        def experts(g, words_of):
            for e in range(EG * g, EG * (g + 1)):
                expert_product(e, *words_of(e))
                if e == 0:
                    turn(e)
                elif e % EG and e != 1:
                    turn(e - 1)
            turn(EG * (g + 1) - 1)

        experts(0, lambda e: (we_w[min(e, 1)], min(e, 1)))
        load_expert_scales(1, tag="we_w0")
        we_w[EG] = load_expert_words("we_w47", EG, EG, tag="z_rows0")
        experts(1, lambda e: (we_w[EG], EG))
        a_t = [load_a(0, "z_rows2"), load_a(1, "z_rows4")]
        slope = [tile("slope%d" % g, [P, PACK, C1], F32) for g in range(G)]
        for g in range(G):
            for t in range(PACK):
                nc.scalar.activation(slope[g][:, t, :], a_t[g][:, t, :], RELU)
        wg_w = tile("wg_w", [P, G, K], U32, "z_rows5")
        nc.sync.dma_start(out=wg_w[:].bitcast(I32), in_=wgt_words[:, 0].rearrange("f p k d -> p f (k d)").bitcast(I32))

        wg_s = tile("wg_s", [P, G, K], U8, "z_rows3")
        for r in range(4):
            nc.sync.dma_start(
                out=wg_s[r:P:32, :, :].bitcast(I32),
                in_=wgt_scales[:, 0, r:16:4, :].rearrange("f q k -> q f k").bitcast(I32),
            )

        window = {}
        woven = [tile("woven%d" % g, [P, C1, PACK], BF16) for g in range(G)]
        codes = {}
        planes = {}
        dx = {}
        rows_out = {}

        def scatter_z(g, t, first, count, tag=None):
            if (g, t) not in window:
                window[g, t] = tile("window%d%d" % (g, t), [P, T], F32, tag)
            nc.vector.tensor_copy(
                window[g, t][:].indirect(offs2_t[:, cols(C1 * g + first, count)]), z_slots[g][:, t, first : first + count]
            )

        def times_slope(g, t):
            nc.gpsimd.tensor_tensor(
                woven[g][:, :, t], slope[g][:, t, :], window[g, t][:, C1 * g : C1 * (g + 1)], MULT
            )

        def group_product(g, tag):
            codes[g] = tile("codes%d" % g, [P, C1], U32, tag)
            planes[g] = tile("planes%d" % g, [P, C1], U8)
            nc.vector.quantize_mx(
                out=codes[g][:].bitcast(FP8X4), scales=planes[g][:], in_=woven[g][:].rearrange("p j t -> p (j t)")
            )
            for b in range(K // P):
                acc = bank("dx_ps%d%d" % (g, b), [P, C1], 2 + b)
                nc.tensor.matmul_mx(
                    out=acc[:],
                    lhsT=wg_w[:, g, P * b : P * (b + 1)].bitcast(FP8X4),
                    lhsT_scale=wg_s[:, g, P * b : P * (b + 1)],
                    rhs=codes[g][:].bitcast(FP8X4),
                    rhs_scale=planes[g][:],
                    start=True,
                    stop=True,
                )
                dx[g, b] = tile("dx%d%d" % (g, b), [P, C1], F32)
                nc.scalar.copy(dx[g, b][:], acc[:])

        def scatter_dx(g, b, tag=None):
            if b not in rows_out:
                rows_out[b] = tile("rows_out%d" % b, [P, T], F32, tag)
            nc.vector.tensor_copy(rows_out[b][:].indirect(offs_t[:, cols(C1 * g, C1)]), dx[g, b][:])

        for first in (0, C2):
            for t in range(PACK):
                scatter_z(0, t, first, C2)
        for t in range(PACK):
            scatter_z(0, t, HALF, HALF)
            if t:
                times_slope(0, t - 1)
        scatter_z(1, 0, 0, C1)
        times_slope(0, PACK - 1)
        scatter_z(1, 1, 0, C1)
        times_slope(1, 0)
        scatter_z(1, 2, 0, C1)
        times_slope(1, 1)
        group_product(0, "window10")
        scatter_z(1, 3, 0, C1, tag="woven0")
        times_slope(1, 2)
        times_slope(1, 3)
        scatter_dx(0, 0)
        group_product(1, "dx00")
        scatter_dx(0, 1, tag="woven1")
        for b in range(K // P):
            scatter_dx(1, b)
            nc.sync.dma_start(out=out[P * b : P * (b + 1), :], in_=rows_out[b][:])
